import numpy as np
import ml_dtypes


def mxq(x, axis, fmt="e4m3"):
    dtype, down = {"e4m3": (ml_dtypes.float8_e4m3fn, 7), "e5m2": (ml_dtypes.float8_e5m2, 14)}[fmt]
    v = np.moveaxis(np.asarray(x, np.float32).astype(ml_dtypes.bfloat16).astype(np.float64), axis, -1)
    blocks = v.reshape(v.shape[:-1] + (-1, 32))
    amax = np.abs(blocks).max(-1, keepdims=True)
    byte = np.maximum(np.where(amax > 0, np.frexp(amax)[1] - 1 + 127, 0) - down, 1)
    scale = np.exp2(byte - 127.0)
    codes = (blocks / scale).astype(np.float32).astype(dtype).astype(np.float64)
    return np.moveaxis((codes * scale).reshape(v.shape), -1, axis)


WIDE = False


def mx_kscale(k):
    if not WIDE:
        return np.ones(k)
    levels = np.array([10, -10, 5, -5, 0])
    if k % 512:
        return np.exp2(np.random.permutation(np.resize(levels, k // 32))).repeat(32)
    a = np.empty((k // 512, 16))
    for p in range(k // 512):
        a[p, :8] = np.random.permutation(np.resize(levels, 8))
        for g in range(8):
            far = levels[np.abs(levels - a[p, g]) >= 10]
            a[p, g + 8] = far[np.random.randint(len(far))]
    return np.exp2(a.ravel()).repeat(32)


def f64(x):
    return np.asarray(x).astype(np.float64)


def striped(idx):
    return np.tile(np.asarray(idx).reshape(-1, 16).T, (8, 1)).astype(np.uint16)


def unstriped(offs):
    return offs[:16].T.reshape(-1).astype(np.int64)


E2M1 = np.array([0.0, 0.5, 1.0, 1.5, 2.0, 3.0, 4.0, 6.0, -0.0, -0.5, -1.0, -1.5, -2.0, -3.0, -4.0, -6.0])


def pack_weight(w, fmt):
    k, n = w.shape
    w = f64(np.asarray(w, np.float32).astype(ml_dtypes.bfloat16)).reshape(k // 32, 32, n)
    amax = np.abs(w).max(1)
    if fmt == "e4m3":
        byte = np.frexp(amax)[1] - 1 + 127 - 7
    else:
        mant, ex = np.frexp(amax / 6.0)
        byte = np.where(mant > 0.5, ex, ex - 1) + 127
    byte = np.clip(np.where(amax > 0, byte, 1), 1, 254)
    scaled = (w * np.exp2(127.0 - byte)[:, None, :]).reshape(k, n).astype(np.float32)
    by_word = np.ascontiguousarray(scaled.reshape(k // 512, 128, 4, n).transpose(0, 1, 3, 2))
    if fmt == "e4m3":
        words = by_word.astype(ml_dtypes.float8_e4m3fn).view(np.uint8)
    else:
        c = by_word.astype(ml_dtypes.float4_e2m1fn).view(np.uint8) & 0xF
        words = (c[..., 0::2] | (c[..., 1::2] << 4)).reshape(k // 512, 128, 2 * n)
    return np.ascontiguousarray(words), np.ascontiguousarray(byte.astype(np.uint8).reshape(k // 512, 16, n))


def unpack_weight(words, scales, fmt):
    g, _, n = scales.shape
    words = np.ascontiguousarray(words).reshape(g, 128, n, -1)
    if fmt == "e4m3":
        vals = words.view(ml_dtypes.float8_e4m3fn).astype(np.float64)
    else:
        nib = np.empty((g, 128, n, 4), np.uint8)
        nib[..., 0::2] = words & 0xF
        nib[..., 1::2] = words >> 4
        vals = E2M1[nib]
    vals = vals * np.repeat(np.exp2(scales.astype(np.float64) - 127.0), 8, axis=1)[..., None]
    return vals.transpose(0, 1, 3, 2).reshape(g * 512, n)


D, E, T, I, Q, G = 512, 512, 2048, 512, 128, 64


def setup_inputs():
    n = np.random.standard_normal
    idx = np.random.permutation(T)[:I]
    fd = mx_kscale(D)
    fe = mx_kscale(E)
    keysp = pack_weight(n((D, T)) / fd[:, None], "e2m1")
    valsp = pack_weight(n((E, T)) / fe[:, None], "e2m1")
    return {
        "query": (n((D, Q)) * 0.6 / np.sqrt(D) * fd[:, None]).astype(np.float32),
        "keys_words": keysp[0],
        "keys_scales": keysp[1],
        "pen": (np.random.uniform(10.0, 40.0, (Q, 1))).astype(np.float32),
        "gout": (n((E, Q)) * 1 / np.sqrt(E) * fe[:, None]).astype(np.float32),
        "vals_words": valsp[0],
        "vals_scales": valsp[1],
        "old": (0.5 * n((Q, T))).astype(np.float32),
        "offs": striped(idx),
    }


def reference(query, keys_words, keys_scales, pen, gout, vals_words, vals_scales, old, offs):
    idx = unstriped(offs)
    keysu = unpack_weight(keys_words, keys_scales, "e2m1")
    valsu = unpack_weight(vals_words, vals_scales, "e2m1")
    queryq = mxq(f64(query), 0, "e4m3")
    keysidxg = keysu[:, idx]
    a = queryq.T @ keysidxg
    p = np.exp(a - np.max(a, axis=1, keepdims=True))
    z = np.sum(p, axis=1, keepdims=True)
    goutq = mxq(f64(gout), 0, "e4m3")
    valsidxg = valsu[:, idx]
    c0 = goutq.T @ valsidxg
    s = p.reshape(Q, G, I // G).sum(axis=2) / z
    ds = f64(pen) * (-1.0) * s * 2.0
    e1 = ds / z
    r1 = np.repeat(e1, I // G, axis=1)
    dz = np.sum(ds * p.reshape(Q, G, I // G).sum(axis=2) / np.square(z) * (-1.0), axis=1, keepdims=True) - np.sum(p * c0, axis=1, keepdims=True) / np.square(z)
    dp = 1.0 / z * c0 + r1 + dz
    da = dp * p
    gs = da * 512.0
    gf = np.zeros((Q, T))
    gf[:, idx] = gs
    y = f64(old) + gf
    return y

@@ -1,0 +1,171 @@
+from contextlib import ExitStack
+
+import concourse.mybir as mybir
+
+F32 = mybir.dt.float32
+BF16 = mybir.dt.bfloat16
+I32 = mybir.dt.int32
+U32 = mybir.dt.uint32
+U16 = mybir.dt.uint16
+U8 = mybir.dt.uint8
+FP8X4 = mybir.dt.float8_e4m3fn_x4
+FP4X4 = mybir.dt.float4_e2m1fn_x4
+ALU = mybir.AluOpType
+ACT = mybir.ActivationFunctionType
+AX = mybir.AxisListType
+
+P = 128
+PACK = 4
+TOKENS = 2048
+SLOTS = 512
+ROWS = 128
+PAGE = 8
+PAGES = SLOTS // PAGE
+GAIN = 512.0
+STORE_WIDTHS = (256, 512, 512, 512, 256)
+
+FLOPS = 2 * 2 * 512 * ROWS * SLOTS
+
+
+def tile_attend_bcrowding_s_kernel(tc, query, keys_words, keys_scales, pen, gout, vals_words, vals_scales, old, offs, out):
+    nc = tc.nc
+    with ExitStack() as ctx:
+        sb = ctx.enter_context(tc.tile_pool(name="sb", bufs=1))
+        ps = ctx.enter_context(tc.psum_pool(name="ps", bufs=1))
+
+        offsets = sb.tile([P, SLOTS // 16], U16, name="offsets")
+        k_words = sb.tile([P, TOKENS], U16, name="k_words", align_bytes=64)
+
+        k_scales = sb.tile([P, TOKENS], U8, name="k_scales", align_bytes=64)
+        v_scales = sb.tile([P, TOKENS], U8, name="v_scales", align_bytes=64)
+        q_raw = sb.tile([P, PACK, ROWS], F32, name="q_raw", tag="query_then_old")
+        pen_col = sb.tile([P, 1], F32, name="pen_col")
+        window = sb.tile([P, TOKENS], F32, name="window")
+
+        def load_scales(tile, rows):
+            for quad in range(4):
+                nc.sync.dma_start(
+                    out=tile[32 * quad : 32 * quad + 4, :].bitcast(I32),
+                    in_=rows[0, 4 * quad : 4 * quad + 4, :].bitcast(I32),
+                )
+
+        def load_rows(tile, rows):
+            nc.sync.dma_start(out=tile[:], in_=rows.rearrange("(p j) w -> p j w", j=PACK))
+
+        nc.gpsimd.memset(k_scales[:].bitcast(I32), 0)
+        nc.vector.memset(v_scales[:].bitcast(I32), 0)
+        nc.vector.memset(window[:], 0.0)
+
+        warm_in = sb.tile([P, 1], F32, name="warm_in", tag="warm_then_gout")
+        warm_out = sb.tile([P, 1], F32, name="warm_out", tag="warm_then_vals", align_bytes=64)
+        nc.gpsimd.memset(warm_in[:], 0.0)
+        nc.scalar.activation(warm_out[:], warm_in[:], ACT.Exp)
+
+        nc.sync.dma_start(offsets[:], offs)
+        nc.sync.dma_start(out=k_words[:].bitcast(I32), in_=keys_words[0].bitcast(I32))
+        load_rows(q_raw, query)
+        load_scales(k_scales, keys_scales)
+        load_scales(v_scales, vals_scales)
+        g_raw = sb.tile([P, PACK, ROWS], F32, name="g_raw", tag="warm_then_gout")
+        load_rows(g_raw, gout)
+        v_words = sb.tile([P, TOKENS], U16, name="v_words", tag="warm_then_vals", align_bytes=64)
+        nc.sync.dma_start(out=v_words[:].bitcast(I32), in_=vals_words[0].bitcast(I32))
+        nc.gpsimd.dma_start(out=pen_col[:], in_=pen)
+
+        pen_up = sb.tile([P, 1], F32, name="pen_up")
+        pen_down = sb.tile([P, 1], F32, name="pen_down")
+        nc.gpsimd.tensor_scalar(pen_up[:], pen_col[:], 2.0, 1.0, ALU.mult, ALU.mult)
+        nc.gpsimd.tensor_scalar(pen_down[:], pen_col[:], -2.0, 1.0, ALU.mult, ALU.mult)
+
+        def interleave(raw, name):
+            grouped = sb.tile([P, ROWS, PACK], BF16, name=name, tag=name, align_bytes=64)
+            nc.scalar.copy(grouped[:], raw[:].rearrange("p j w -> p w j"))
+            return grouped
+
+        def quantise(grouped, name):
+            codes = sb.tile([P, ROWS], U32, name=name + "_codes", align_bytes=64)
+            scales = sb.tile([P, ROWS], U8, name=name + "_scales", align_bytes=64)
+            nc.vector.quantize_mx(
+                out=codes[:].bitcast(FP8X4), scales=scales[:], in_=grouped[:].rearrange("p w j -> p (w j)")
+            )
+            return codes, scales
+
+        def gather(pool_tile, dtype, name, tag):
+            picked = sb.tile([P, SLOTS], dtype, name=name, tag=tag, align_bytes=64)
+            nc.vector.tensor_copy(picked[:], pool_tile[:].indirect(offsets[:]))
+            return picked
+
+        def product(codes, scales, words, word_scales, name):
+            bank = ps.tile([ROWS, SLOTS], F32, name=name)
+            nc.tensor.matmul_mx(
+                out=bank[:],
+                lhsT=codes[:].bitcast(FP8X4),
+                lhsT_scale=scales[:],
+                rhs=words[:].bitcast(FP4X4),
+                rhs_scale=word_scales[:],
+                start=True,
+                stop=True,
+            )
+            return bank
+
+        q_grouped = interleave(q_raw, "q_grouped")
+        g_grouped = interleave(g_raw, "g_grouped")
+        total = sb.tile([P, TOKENS], F32, name="total", tag="query_then_old")
+        nc.sync.dma_start(out=total[:], in_=old)
+
+        k_words_g = gather(k_words, U16, "k_words_g", "picked_words")
+        k_scales_g = gather(k_scales, U8, "k_scales_g", "picked_key_scales")
+        q_codes, q_scales = quantise(q_grouped, "q")
+        scores = product(q_codes, q_scales, k_words_g, k_scales_g, "scores")
+
+        v_scales_g = gather(v_scales, U8, "v_scales_g", "q_grouped")
+        neg_max = sb.tile([P, 1], F32, name="neg_max")
+        nc.vector.tensor_reduce(neg_max[:], scores[:], AX.X, ALU.max, negate=True)
+        p = sb.tile([P, SLOTS], F32, name="p", tag="warm_then_gout")
+        z = sb.tile([P, 1], F32, name="z")
+        nc.scalar.activation(p[:], scores[:], ACT.Exp, bias=neg_max[:], accum_out=z[:])
+
+        g_codes, g_scales = quantise(g_grouped, "g")
+        v_words_g = gather(v_words, U16, "v_words_g", "picked_words")
+        c0 = product(g_codes, g_scales, v_words_g, v_scales_g, "c0")
+
+        inv_z = sb.tile([P, 1], F32, name="inv_z", tag="warm_then_vals", align_bytes=64)
+        nc.vector.reciprocal(inv_z[:], z[:])
+        page_sum = sb.tile([P, PAGES], F32, name="page_sum")
+        nc.vector.tensor_reduce(page_sum[:], p[:].rearrange("p (g j) -> p g j", j=PAGE), AX.X, ALU.add)
+
+        weight = sb.tile([P, SLOTS], F32, name="weight")
+        nc.gpsimd.tensor_scalar(weight[:], p[:], inv_z[:], GAIN, ALU.mult, ALU.mult)
+
+        slope = sb.tile([P, 1], F32, name="slope")
+        nc.scalar.activation(slope[:], inv_z[:], ACT.Copy, scale=pen_down[:])
+        share_sq = sb.tile([P, PAGES], F32, name="share_sq")
+        crowding = sb.tile([P, 1], F32, name="crowding")
+        nc.scalar.activation(share_sq[:], page_sum[:], ACT.Square, scale=inv_z[:], accum_out=crowding[:])
+        shift = sb.tile([P, 1], F32, name="shift")
+        nc.scalar.activation(shift[:], crowding[:], ACT.Copy, scale=pen_up[:])
+        page_term = sb.tile([P, PAGES], F32, name="page_term")
+        nc.scalar.activation(page_term[:], page_sum[:], ACT.Identity, scale=slope[:], bias=shift[:])
+
+        weighted = sb.tile([P, SLOTS], F32, name="weighted")
+        mean_c0 = sb.tile([P, 1], F32, name="mean_c0")
+        nc.vector.scalar_tensor_tensor(
+            weighted[:], c0[:], inv_z[:], p[:], ALU.mult, ALU.mult, accum_out=mean_c0[:]
+        )
+        centred = sb.tile([P, SLOTS], F32, name="centred")
+        nc.vector.scalar_tensor_tensor(
+            centred[:].rearrange("p (g j) -> p g j", j=PAGE),
+            c0[:].rearrange("p (g j) -> p g j", j=PAGE),
+            mean_c0[:],
+            page_term[:].unsqueeze(2).to_broadcast([P, PAGES, PAGE]),
+            ALU.subtract,
+            ALU.add,
+        )
+        nc.vector.tensor_tensor(window[:].indirect(offsets[:]), centred[:], weight[:], ALU.mult)
+
+        start = 0
+        for width in STORE_WIDTHS:
+            cols = slice(start, start + width)
+            nc.vector.tensor_tensor(total[:, cols], total[:, cols], window[:, cols], ALU.add)
+            nc.sync.dma_start(out=out[:, cols], in_=total[:, cols])
+            start = start + width

@@ -22,7 +22,7 @@ ROWS = 128
 PAGE = 8
 PAGES = SLOTS // PAGE
 GAIN = 512.0
-STORE_WIDTHS = (256, 512, 512, 512, 256)
+STORE_WIDTHS = (640, 512, 384, 320, 192)
 
 FLOPS = 2 * 2 * 512 * ROWS * SLOTS
 
@@ -37,7 +37,7 @@ def tile_attend_bcrowding_s_kernel(tc, query, keys_words, keys_scales, pen, gout
         k_words = sb.tile([P, TOKENS], U16, name="k_words", align_bytes=64)
 
         k_scales = sb.tile([P, TOKENS], U8, name="k_scales", align_bytes=64)
-        v_scales = sb.tile([P, TOKENS], U8, name="v_scales", align_bytes=64)
+        v_scales = sb.tile([P, TOKENS], U8, name="v_scales", tag="val_scales_then_inv_z", align_bytes=64)
         q_raw = sb.tile([P, PACK, ROWS], F32, name="q_raw", tag="query_then_old")
         pen_col = sb.tile([P, 1], F32, name="pen_col")
         window = sb.tile([P, TOKENS], F32, name="window")
@@ -52,24 +52,24 @@ def tile_attend_bcrowding_s_kernel(tc, query, keys_words, keys_scales, pen, gout
         def load_rows(tile, rows):
             nc.sync.dma_start(out=tile[:], in_=rows.rearrange("(p j) w -> p j w", j=PACK))
 
-        nc.gpsimd.memset(k_scales[:].bitcast(I32), 0)
-        nc.vector.memset(v_scales[:].bitcast(I32), 0)
+        nc.vector.memset(k_scales[:].bitcast(I32), 0)
         nc.vector.memset(window[:], 0.0)
+        nc.vector.memset(v_scales[:].bitcast(I32), 0)
 
         warm_in = sb.tile([P, 1], F32, name="warm_in", tag="warm_then_gout")
         warm_out = sb.tile([P, 1], F32, name="warm_out", tag="warm_then_vals", align_bytes=64)
         nc.gpsimd.memset(warm_in[:], 0.0)
         nc.scalar.activation(warm_out[:], warm_in[:], ACT.Exp)
 
-        nc.sync.dma_start(offsets[:], offs)
         nc.sync.dma_start(out=k_words[:].bitcast(I32), in_=keys_words[0].bitcast(I32))
+        nc.sync.dma_start(offsets[:], offs)
         load_rows(q_raw, query)
         load_scales(k_scales, keys_scales)
-        load_scales(v_scales, vals_scales)
-        g_raw = sb.tile([P, PACK, ROWS], F32, name="g_raw", tag="warm_then_gout")
-        load_rows(g_raw, gout)
         v_words = sb.tile([P, TOKENS], U16, name="v_words", tag="warm_then_vals", align_bytes=64)
         nc.sync.dma_start(out=v_words[:].bitcast(I32), in_=vals_words[0].bitcast(I32))
+        g_raw = sb.tile([P, PACK, ROWS], F32, name="g_raw", tag="warm_then_gout")
+        load_rows(g_raw, gout)
+        load_scales(v_scales, vals_scales)
         nc.gpsimd.dma_start(out=pen_col[:], in_=pen)
 
         pen_up = sb.tile([P, 1], F32, name="pen_up")
@@ -90,67 +90,75 @@ def tile_attend_bcrowding_s_kernel(tc, query, keys_words, keys_scales, pen, gout
             )
             return codes, scales
 
-        def gather(pool_tile, dtype, name, tag):
+        def gather(pool_tile, dtype, name, tag, pieces=1):
             picked = sb.tile([P, SLOTS], dtype, name=name, tag=tag, align_bytes=64)
-            nc.vector.tensor_copy(picked[:], pool_tile[:].indirect(offsets[:]))
+            width = SLOTS // pieces
+            for piece in range(pieces):
+                entries = offsets[:, piece * width // 16 : (piece + 1) * width // 16]
+                nc.vector.tensor_copy(picked[:, piece * width : (piece + 1) * width], pool_tile[:].indirect(entries))
             return picked
 
-        def product(codes, scales, words, word_scales, name):
+        def product(codes, scales, words, word_scales, name, pieces=1):
             bank = ps.tile([ROWS, SLOTS], F32, name=name)
-            nc.tensor.matmul_mx(
-                out=bank[:],
-                lhsT=codes[:].bitcast(FP8X4),
-                lhsT_scale=scales[:],
-                rhs=words[:].bitcast(FP4X4),
-                rhs_scale=word_scales[:],
-                start=True,
-                stop=True,
-            )
+            width = SLOTS // pieces
+            for piece in range(pieces):
+                cols = slice(piece * width, (piece + 1) * width)
+                nc.tensor.matmul_mx(
+                    out=bank[:, cols],
+                    lhsT=codes[:].bitcast(FP8X4),
+                    lhsT_scale=scales[:],
+                    rhs=words[:, cols].bitcast(FP4X4),
+                    rhs_scale=word_scales[:, cols],
+                    start=True,
+                    stop=True,
+                )
             return bank
 
         q_grouped = interleave(q_raw, "q_grouped")
         g_grouped = interleave(g_raw, "g_grouped")
-        total = sb.tile([P, TOKENS], F32, name="total", tag="query_then_old")
-        nc.sync.dma_start(out=total[:], in_=old)
+
 
         k_words_g = gather(k_words, U16, "k_words_g", "picked_words")
         k_scales_g = gather(k_scales, U8, "k_scales_g", "picked_key_scales")
         q_codes, q_scales = quantise(q_grouped, "q")
         scores = product(q_codes, q_scales, k_words_g, k_scales_g, "scores")
+        total = sb.tile([P, TOKENS], F32, name="total", tag="picked_key_scales", align_bytes=64)
+        nc.sync.dma_start(out=total[:], in_=old)
 
-        v_scales_g = gather(v_scales, U8, "v_scales_g", "q_grouped")
-        neg_max = sb.tile([P, 1], F32, name="neg_max")
+        v_words_g = gather(v_words, U16, "v_words_g", "picked_val_words")
+        g_codes, g_scales = quantise(g_grouped, "g")
+        neg_max = sb.tile([P, 1], F32, name="neg_max", tag="warm_then_gout")
         nc.vector.tensor_reduce(neg_max[:], scores[:], AX.X, ALU.max, negate=True)
-        p = sb.tile([P, SLOTS], F32, name="p", tag="warm_then_gout")
+        p = sb.tile([P, SLOTS], F32, name="p")
         z = sb.tile([P, 1], F32, name="z")
         nc.scalar.activation(p[:], scores[:], ACT.Exp, bias=neg_max[:], accum_out=z[:])
 
-        g_codes, g_scales = quantise(g_grouped, "g")
-        v_words_g = gather(v_words, U16, "v_words_g", "picked_words")
-        c0 = product(g_codes, g_scales, v_words_g, v_scales_g, "c0")
+        v_scales_g = gather(v_scales, U8, "v_scales_g", "g_grouped", pieces=2)
+        c0 = product(g_codes, g_scales, v_words_g, v_scales_g, "c0", pieces=2)
 
-        inv_z = sb.tile([P, 1], F32, name="inv_z", tag="warm_then_vals", align_bytes=64)
-        nc.vector.reciprocal(inv_z[:], z[:])
-        page_sum = sb.tile([P, PAGES], F32, name="page_sum")
-        nc.vector.tensor_reduce(page_sum[:], p[:].rearrange("p (g j) -> p g j", j=PAGE), AX.X, ALU.add)
+        sums = sb.tile([P, PAGES + 1], F32, name="sums")
+        page_sum = sums[:, 0:PAGES]
+        inv_z = sums[:, PAGES : PAGES + 1]
+        nc.vector.reciprocal(inv_z, z[:])
+        nc.vector.tensor_reduce(page_sum, p[:].rearrange("p (g j) -> p g j", j=PAGE), AX.X, ALU.add)
 
         weight = sb.tile([P, SLOTS], F32, name="weight")
-        nc.gpsimd.tensor_scalar(weight[:], p[:], inv_z[:], GAIN, ALU.mult, ALU.mult)
+        nc.gpsimd.tensor_scalar(weight[:], p[:], inv_z, GAIN, ALU.mult, ALU.mult)
 
         slope = sb.tile([P, 1], F32, name="slope")
-        nc.scalar.activation(slope[:], inv_z[:], ACT.Copy, scale=pen_down[:])
+        nc.scalar.activation(slope[:], inv_z, ACT.Copy, scale=pen_down[:])
         share_sq = sb.tile([P, PAGES], F32, name="share_sq")
         crowding = sb.tile([P, 1], F32, name="crowding")
-        nc.scalar.activation(share_sq[:], page_sum[:], ACT.Square, scale=inv_z[:], accum_out=crowding[:])
+        nc.scalar.activation(share_sq[:], page_sum, ACT.Square, scale=inv_z, accum_out=crowding[:])
         shift = sb.tile([P, 1], F32, name="shift")
         nc.scalar.activation(shift[:], crowding[:], ACT.Copy, scale=pen_up[:])
         page_term = sb.tile([P, PAGES], F32, name="page_term")
-        nc.scalar.activation(page_term[:], page_sum[:], ACT.Identity, scale=slope[:], bias=shift[:])
+        nc.scalar.activation(page_term[:], page_sum, ACT.Identity, scale=slope[:], bias=shift[:])
 
         weighted = sb.tile([P, SLOTS], F32, name="weighted")
         mean_c0 = sb.tile([P, 1], F32, name="mean_c0")
         nc.vector.scalar_tensor_tensor(
-            weighted[:], c0[:], inv_z[:], p[:], ALU.mult, ALU.mult, accum_out=mean_c0[:]
+            weighted[:], c0[:], inv_z, p[:], ALU.mult, ALU.mult, accum_out=mean_c0[:]
         )
         centred = sb.tile([P, SLOTS], F32, name="centred")
         nc.vector.scalar_tensor_tensor(

@@ -22,7 +22,7 @@ ROWS = 128
 PAGE = 8
 PAGES = SLOTS // PAGE
 GAIN = 512.0
-STORE_WIDTHS = (640, 512, 384, 320, 192)
+STORE_WIDTHS = (256, 512, 448, 384, 256, 192)
 
 FLOPS = 2 * 2 * 512 * ROWS * SLOTS
 
@@ -39,7 +39,6 @@ def tile_attend_bcrowding_s_kernel(tc, query, keys_words, keys_scales, pen, gout
         k_scales = sb.tile([P, TOKENS], U8, name="k_scales", align_bytes=64)
         v_scales = sb.tile([P, TOKENS], U8, name="v_scales", tag="val_scales_then_inv_z", align_bytes=64)
         q_raw = sb.tile([P, PACK, ROWS], F32, name="q_raw", tag="query_then_old")
-        pen_col = sb.tile([P, 1], F32, name="pen_col")
         window = sb.tile([P, TOKENS], F32, name="window")
 
         def load_scales(tile, rows):
@@ -60,6 +59,11 @@ def tile_attend_bcrowding_s_kernel(tc, query, keys_words, keys_scales, pen, gout
         warm_out = sb.tile([P, 1], F32, name="warm_out", tag="warm_then_vals", align_bytes=64)
         nc.gpsimd.memset(warm_in[:], 0.0)
         nc.scalar.activation(warm_out[:], warm_in[:], ACT.Exp)
+        twos = sb.tile([P, 2], F32, name="twos")
+        nc.gpsimd.memset(twos[:, 0:1], 2.0)
+        nc.gpsimd.memset(twos[:, 1:2], -2.0)
+        factors = sb.tile([P, 3], F32, name="factors")
+        nc.gpsimd.memset(factors[:, 2:3], GAIN)
 
         nc.sync.dma_start(out=k_words[:].bitcast(I32), in_=keys_words[0].bitcast(I32))
         nc.sync.dma_start(offsets[:], offs)
@@ -70,12 +74,7 @@ def tile_attend_bcrowding_s_kernel(tc, query, keys_words, keys_scales, pen, gout
         g_raw = sb.tile([P, PACK, ROWS], F32, name="g_raw", tag="warm_then_gout")
         load_rows(g_raw, gout)
         load_scales(v_scales, vals_scales)
-        nc.gpsimd.dma_start(out=pen_col[:], in_=pen)
 
-        pen_up = sb.tile([P, 1], F32, name="pen_up")
-        pen_down = sb.tile([P, 1], F32, name="pen_down")
-        nc.gpsimd.tensor_scalar(pen_up[:], pen_col[:], 2.0, 1.0, ALU.mult, ALU.mult)
-        nc.gpsimd.tensor_scalar(pen_down[:], pen_col[:], -2.0, 1.0, ALU.mult, ALU.mult)
 
         def interleave(raw, name):
             grouped = sb.tile([P, ROWS, PACK], BF16, name=name, tag=name, align_bytes=64)
@@ -115,7 +114,10 @@ def tile_attend_bcrowding_s_kernel(tc, query, keys_words, keys_scales, pen, gout
             return bank
 
         q_grouped = interleave(q_raw, "q_grouped")
+        pen_col = sb.tile([P, 1], F32, name="pen_col", tag="query_then_old")
+        nc.sync.dma_start(out=pen_col[:], in_=pen)
         g_grouped = interleave(g_raw, "g_grouped")
+        nc.scalar.activation(factors[:, 0:2], twos[:], ACT.Copy, scale=pen_col[:])
 
 
         k_words_g = gather(k_words, U16, "k_words_g", "picked_words")
@@ -142,18 +144,17 @@ def tile_attend_bcrowding_s_kernel(tc, query, keys_words, keys_scales, pen, gout
         nc.vector.reciprocal(inv_z, z[:])
         nc.vector.tensor_reduce(page_sum, p[:].rearrange("p (g j) -> p g j", j=PAGE), AX.X, ALU.add)
 
-        weight = sb.tile([P, SLOTS], F32, name="weight")
-        nc.gpsimd.tensor_scalar(weight[:], p[:], inv_z, GAIN, ALU.mult, ALU.mult)
-
-        slope = sb.tile([P, 1], F32, name="slope")
-        nc.scalar.activation(slope[:], inv_z, ACT.Copy, scale=pen_down[:])
+        over_z = sb.tile([P, 2], F32, name="over_z")
+        nc.scalar.activation(over_z[:], factors[:, 1:3], ACT.Copy, scale=inv_z)
         share_sq = sb.tile([P, PAGES], F32, name="share_sq")
-        crowding = sb.tile([P, 1], F32, name="crowding")
+        crowding = sb.tile([P, 1], F32, name="crowding", tag="crowding_then_weight")
         nc.scalar.activation(share_sq[:], page_sum, ACT.Square, scale=inv_z, accum_out=crowding[:])
         shift = sb.tile([P, 1], F32, name="shift")
-        nc.scalar.activation(shift[:], crowding[:], ACT.Copy, scale=pen_up[:])
+        nc.scalar.activation(shift[:], crowding[:], ACT.Copy, scale=factors[:, 0:1])
         page_term = sb.tile([P, PAGES], F32, name="page_term")
-        nc.scalar.activation(page_term[:], page_sum, ACT.Identity, scale=slope[:], bias=shift[:])
+        nc.scalar.activation(page_term[:], page_sum, ACT.Identity, scale=over_z[:, 0:1], bias=shift[:])
+        weight = sb.tile([P, SLOTS], F32, name="weight", tag="crowding_then_weight")
+        nc.scalar.activation(weight[:], p[:], ACT.Copy, scale=over_z[:, 1:2])
 
         weighted = sb.tile([P, SLOTS], F32, name="weighted")
         mean_c0 = sb.tile([P, 1], F32, name="mean_c0")

@@ -55,10 +55,6 @@ def tile_attend_bcrowding_s_kernel(tc, query, keys_words, keys_scales, pen, gout
         nc.vector.memset(window[:], 0.0)
         nc.vector.memset(v_scales[:].bitcast(I32), 0)
 
-        warm_in = sb.tile([P, 1], F32, name="warm_in", tag="warm_then_gout")
-        warm_out = sb.tile([P, 1], F32, name="warm_out", tag="warm_then_vals", align_bytes=64)
-        nc.gpsimd.memset(warm_in[:], 0.0)
-        nc.scalar.activation(warm_out[:], warm_in[:], ACT.Exp)
         twos = sb.tile([P, 2], F32, name="twos")
         nc.gpsimd.memset(twos[:, 0:1], 2.0)
         nc.gpsimd.memset(twos[:, 1:2], -2.0)

from contextlib import ExitStack

import concourse.mybir as mybir

F32 = mybir.dt.float32
BF16 = mybir.dt.bfloat16
I32 = mybir.dt.int32
U32 = mybir.dt.uint32
U16 = mybir.dt.uint16
U8 = mybir.dt.uint8
FP8X4 = mybir.dt.float8_e4m3fn_x4
FP4X4 = mybir.dt.float4_e2m1fn_x4
ALU = mybir.AluOpType
ACT = mybir.ActivationFunctionType
AX = mybir.AxisListType

P = 128
PACK = 4
TOKENS = 2048
SLOTS = 512
ROWS = 128
PAGE = 8
PAGES = SLOTS // PAGE
GAIN = 512.0
STORE_WIDTHS = (256, 512, 448, 384, 256, 192)

FLOPS = 2 * 2 * 512 * ROWS * SLOTS


def tile_attend_bcrowding_s_kernel(tc, query, keys_words, keys_scales, pen, gout, vals_words, vals_scales, old, offs, out):
    nc = tc.nc
    with ExitStack() as ctx:
        sb = ctx.enter_context(tc.tile_pool(name="sb", bufs=1))
        ps = ctx.enter_context(tc.psum_pool(name="ps", bufs=1))

        offsets = sb.tile([P, SLOTS // 16], U16, name="offsets")
        k_words = sb.tile([P, TOKENS], U16, name="k_words", align_bytes=64)

        k_scales = sb.tile([P, TOKENS], U8, name="k_scales", align_bytes=64)
        v_scales = sb.tile([P, TOKENS], U8, name="v_scales", tag="val_scales_then_inv_z", align_bytes=64)
        q_raw = sb.tile([P, PACK, ROWS], F32, name="q_raw", tag="query_then_old")
        window = sb.tile([P, TOKENS], F32, name="window")

        def load_scales(tile, rows):
            for quad in range(4):
                nc.sync.dma_start(
                    out=tile[32 * quad : 32 * quad + 4, :].bitcast(I32),
                    in_=rows[0, 4 * quad : 4 * quad + 4, :].bitcast(I32),
                )

        def load_rows(tile, rows):
            nc.sync.dma_start(out=tile[:], in_=rows.rearrange("(p j) w -> p j w", j=PACK))

        nc.vector.memset(k_scales[:].bitcast(I32), 0)
        nc.vector.memset(window[:], 0.0)
        nc.vector.memset(v_scales[:].bitcast(I32), 0)

        twos = sb.tile([P, 2], F32, name="twos")
        nc.gpsimd.memset(twos[:, 0:1], 2.0)
        nc.gpsimd.memset(twos[:, 1:2], -2.0)
        factors = sb.tile([P, 3], F32, name="factors")
        nc.gpsimd.memset(factors[:, 2:3], GAIN)

        nc.sync.dma_start(out=k_words[:].bitcast(I32), in_=keys_words[0].bitcast(I32))
        nc.sync.dma_start(offsets[:], offs)
        load_rows(q_raw, query)
        load_scales(k_scales, keys_scales)
        v_words = sb.tile([P, TOKENS], U16, name="v_words", tag="warm_then_vals", align_bytes=64)
        nc.sync.dma_start(out=v_words[:].bitcast(I32), in_=vals_words[0].bitcast(I32))
        g_raw = sb.tile([P, PACK, ROWS], F32, name="g_raw", tag="warm_then_gout")
        load_rows(g_raw, gout)
        load_scales(v_scales, vals_scales)


        def interleave(raw, name):
            grouped = sb.tile([P, ROWS, PACK], BF16, name=name, tag=name, align_bytes=64)
            nc.scalar.copy(grouped[:], raw[:].rearrange("p j w -> p w j"))
            return grouped

        def quantise(grouped, name):
            codes = sb.tile([P, ROWS], U32, name=name + "_codes", align_bytes=64)
            scales = sb.tile([P, ROWS], U8, name=name + "_scales", align_bytes=64)
            nc.vector.quantize_mx(
                out=codes[:].bitcast(FP8X4), scales=scales[:], in_=grouped[:].rearrange("p w j -> p (w j)")
            )
            return codes, scales

        def gather(pool_tile, dtype, name, tag, pieces=1):
            picked = sb.tile([P, SLOTS], dtype, name=name, tag=tag, align_bytes=64)
            width = SLOTS // pieces
            for piece in range(pieces):
                entries = offsets[:, piece * width // 16 : (piece + 1) * width // 16]
                nc.vector.tensor_copy(picked[:, piece * width : (piece + 1) * width], pool_tile[:].indirect(entries))
            return picked

        def product(codes, scales, words, word_scales, name, pieces=1):
            bank = ps.tile([ROWS, SLOTS], F32, name=name)
            width = SLOTS // pieces
            for piece in range(pieces):
                cols = slice(piece * width, (piece + 1) * width)
                nc.tensor.matmul_mx(
                    out=bank[:, cols],
                    lhsT=codes[:].bitcast(FP8X4),
                    lhsT_scale=scales[:],
                    rhs=words[:, cols].bitcast(FP4X4),
                    rhs_scale=word_scales[:, cols],
                    start=True,
                    stop=True,
                )
            return bank

        q_grouped = interleave(q_raw, "q_grouped")
        pen_col = sb.tile([P, 1], F32, name="pen_col", tag="query_then_old")
        nc.sync.dma_start(out=pen_col[:], in_=pen)
        g_grouped = interleave(g_raw, "g_grouped")
        nc.scalar.activation(factors[:, 0:2], twos[:], ACT.Copy, scale=pen_col[:])


        k_words_g = gather(k_words, U16, "k_words_g", "picked_words")
        k_scales_g = gather(k_scales, U8, "k_scales_g", "picked_key_scales")
        q_codes, q_scales = quantise(q_grouped, "q")
        scores = product(q_codes, q_scales, k_words_g, k_scales_g, "scores")
        total = sb.tile([P, TOKENS], F32, name="total", tag="picked_key_scales", align_bytes=64)
        nc.sync.dma_start(out=total[:], in_=old)

        v_words_g = gather(v_words, U16, "v_words_g", "picked_val_words")
        g_codes, g_scales = quantise(g_grouped, "g")
        neg_max = sb.tile([P, 1], F32, name="neg_max", tag="warm_then_gout")
        nc.vector.tensor_reduce(neg_max[:], scores[:], AX.X, ALU.max, negate=True)
        p = sb.tile([P, SLOTS], F32, name="p")
        z = sb.tile([P, 1], F32, name="z")
        nc.scalar.activation(p[:], scores[:], ACT.Exp, bias=neg_max[:], accum_out=z[:])

        v_scales_g = gather(v_scales, U8, "v_scales_g", "g_grouped", pieces=2)
        c0 = product(g_codes, g_scales, v_words_g, v_scales_g, "c0", pieces=2)

        sums = sb.tile([P, PAGES + 1], F32, name="sums")
        page_sum = sums[:, 0:PAGES]
        inv_z = sums[:, PAGES : PAGES + 1]
        nc.vector.reciprocal(inv_z, z[:])
        nc.vector.tensor_reduce(page_sum, p[:].rearrange("p (g j) -> p g j", j=PAGE), AX.X, ALU.add)

        over_z = sb.tile([P, 2], F32, name="over_z")
        nc.scalar.activation(over_z[:], factors[:, 1:3], ACT.Copy, scale=inv_z)
        share_sq = sb.tile([P, PAGES], F32, name="share_sq")
        crowding = sb.tile([P, 1], F32, name="crowding", tag="crowding_then_weight")
        nc.scalar.activation(share_sq[:], page_sum, ACT.Square, scale=inv_z, accum_out=crowding[:])
        shift = sb.tile([P, 1], F32, name="shift")
        nc.scalar.activation(shift[:], crowding[:], ACT.Copy, scale=factors[:, 0:1])
        page_term = sb.tile([P, PAGES], F32, name="page_term")
        nc.scalar.activation(page_term[:], page_sum, ACT.Identity, scale=over_z[:, 0:1], bias=shift[:])
        weight = sb.tile([P, SLOTS], F32, name="weight", tag="crowding_then_weight")
        nc.scalar.activation(weight[:], p[:], ACT.Copy, scale=over_z[:, 1:2])

        weighted = sb.tile([P, SLOTS], F32, name="weighted")
        mean_c0 = sb.tile([P, 1], F32, name="mean_c0")
        nc.vector.scalar_tensor_tensor(
            weighted[:], c0[:], inv_z, p[:], ALU.mult, ALU.mult, accum_out=mean_c0[:]
        )
        centred = sb.tile([P, SLOTS], F32, name="centred")
        nc.vector.scalar_tensor_tensor(
            centred[:].rearrange("p (g j) -> p g j", j=PAGE),
            c0[:].rearrange("p (g j) -> p g j", j=PAGE),
            mean_c0[:],
            page_term[:].unsqueeze(2).to_broadcast([P, PAGES, PAGE]),
            ALU.subtract,
            ALU.add,
        )
        nc.vector.tensor_tensor(window[:].indirect(offsets[:]), centred[:], weight[:], ALU.mult)

        start = 0
        for width in STORE_WIDTHS:
            cols = slice(start, start + width)
            nc.vector.tensor_tensor(total[:, cols], total[:, cols], window[:, cols], ALU.add)
            nc.sync.dma_start(out=out[:, cols], in_=total[:, cols])
            start = start + width
